import numpy as np
import ml_dtypes


def mxq(x, axis, fmt="e4m3"):
    dtype, down = {"e4m3": (ml_dtypes.float8_e4m3fn, 7), "e5m2": (ml_dtypes.float8_e5m2, 14)}[fmt]
    v = np.moveaxis(np.asarray(x, np.float32).astype(ml_dtypes.bfloat16).astype(np.float64), axis, -1)
    blocks = v.reshape(v.shape[:-1] + (-1, 32))
    amax = np.abs(blocks).max(-1, keepdims=True)
    byte = np.maximum(np.where(amax > 0, np.frexp(amax)[1] - 1 + 127, 0) - down, 1)
    scale = np.exp2(byte - 127.0)
    codes = (blocks / scale).astype(np.float32).astype(dtype).astype(np.float64)
    return np.moveaxis((codes * scale).reshape(v.shape), -1, axis)


WIDE = False


def mx_kscale(k):
    if not WIDE:
        return np.ones(k)
    levels = np.array([10, -10, 5, -5, 0])
    if k % 512:
        return np.exp2(np.random.permutation(np.resize(levels, k // 32))).repeat(32)
    a = np.empty((k // 512, 16))
    for p in range(k // 512):
        a[p, :8] = np.random.permutation(np.resize(levels, 8))
        for g in range(8):
            far = levels[np.abs(levels - a[p, g]) >= 10]
            a[p, g + 8] = far[np.random.randint(len(far))]
    return np.exp2(a.ravel()).repeat(32)


def f64(x):
    return np.asarray(x).astype(np.float64)


def striped(idx):
    return np.tile(idx.reshape(-1, 16).T, (8, 1)).astype(np.uint16)


def unstriped(offs):
    return offs[:16].T.reshape(-1).astype(np.int64)


def pack_weight(w):
    k, n = w.shape
    w = f64(np.asarray(w, np.float32).astype(ml_dtypes.bfloat16)).reshape(k // 32, 32, n)
    amax = np.abs(w).max(1)
    byte = np.clip(np.where(amax > 0, np.frexp(amax)[1] - 1 + 127 - 7, 1), 1, 254)
    scaled = (w * np.exp2(127.0 - byte)[:, None, :]).reshape(k, n).astype(np.float32)
    words = np.ascontiguousarray(scaled.reshape(k // 512, 128, 4, n).transpose(0, 1, 3, 2)).astype(ml_dtypes.float8_e4m3fn).view(np.uint8)
    return words, np.ascontiguousarray(byte.astype(np.uint8).reshape(k // 512, 16, n))


def unpack_weight(words, scales):
    g, p, n, _ = words.shape
    vals = np.ascontiguousarray(words).view(ml_dtypes.float8_e4m3fn).astype(np.float64) * np.repeat(np.exp2(scales.astype(np.float64) - 127.0), 8, axis=1)[..., None]
    return vals.transpose(0, 1, 3, 2).reshape(g * 512, n)


def silu(v):
    return v / (1.0 + np.exp(-np.maximum(v, -700.0)))


K, T, H, N, J, U = 1024, 1024, 512, 128, 512, 2048


def setup_inputs():
    n = np.random.standard_normal
    s = mx_kscale(K)[:, None]
    u = mx_kscale(H)
    r = mx_kscale(J)[:, None]
    packed_xT = pack_weight(n((K, T)) * s)
    packed_w2 = pack_weight(n((H, N)) / np.sqrt(2 * H) / u[:, None])
    return {
        "x_words": packed_xT[0],
        "x_scales": packed_xT[1],
        "aT": (n((J, U)) * r).astype(np.float32),
        "w1": (n((K, H)) / np.sqrt(K) / s * u).astype(np.float32),
        "w3": (n((J, H)) / np.sqrt(J) / r).astype(np.float32),
        "w2_words": packed_w2[0],
        "w2_scales": packed_w2[1],
        "pos1": striped(np.random.permutation(T)),
        "pos2": striped(np.random.permutation(T)),
    }


def reference(x_words, x_scales, aT, w1, w3, w2_words, w2_scales, pos1, pos2):
    xq = unpack_weight(x_words, x_scales)
    h = silu(mxq(f64(w1), 0, "e4m3").T @ xq)
    f = mxq(f64(w3), 0, "e4m3").T @ mxq(f64(aT), 0, "e4m3")
    z = h[:, unstriped(pos1)] * f[:, :T] + h[:, unstriped(pos2)] * f[:, T:2 * T]
    return silu(unpack_weight(w2_words, w2_scales).T @ mxq(z, 0, "e4m3"))

@@ -1,0 +1,289 @@
+from contextlib import ExitStack
+
+import concourse.mybir as mybir
+from concourse.masks import make_identity
+
+K, T, H, N, J = 1024, 1024, 512, 128, 512
+D = 2
+FLOPS = 2 * (K * H * T + J * H * D * T + H * N * T)
+
+F32 = mybir.dt.float32
+BF16 = mybir.dt.bfloat16
+I32 = mybir.dt.int32
+U32 = mybir.dt.uint32
+U16 = mybir.dt.uint16
+U8 = mybir.dt.uint8
+FP8X4 = mybir.dt.float8_e4m3fn_x4
+SILU = mybir.ActivationFunctionType.Silu
+MULT = mybir.AluOpType.mult
+
+P = 128
+PACK = 4
+K_PASS = P * PACK
+BANK = 512
+PASSES = K // K_PASS
+TILES = H // P
+WIDTHS = (256,256,256,128,128)
+STARTS = tuple(sum(WIDTHS[:c]) for c in range(len(WIDTHS)))
+CHUNKS = len(WIDTHS)
+ON_VECTOR = (256,512,0,0,0)
+W3_ON_VECTOR = ()
+HALVES = T // BANK
+LIST_ROWS = 16
+
+
+def tile_picked_wdime_silu_l_kernel(tc, x_words, x_scales, aT, w1, w3, w2_words, w2_scales, pos1, pos2, out):
+    nc = tc.nc
+    with ExitStack() as ctx:
+        sb = ctx.enter_context(tc.tile_pool(name="sb", bufs=1))
+        ps = ctx.enter_context(tc.psum_pool(name="ps", bufs=1))
+
+        def tile(name, width, dtype):
+            return sb.tile([P, width], dtype, name=name, align_bytes=64)
+
+        banks = [ps.tile([P, BANK], F32, name="bank%d" % b) for b in range(8)]
+
+        x_plane = tile("x_plane", T, U8)
+        w2_plane = tile("w2_plane", N, U8)
+        nc.gpsimd.memset(x_plane[:].bitcast(U32), 0)
+        nc.gpsimd.memset(w2_plane[:].bitcast(U32), 0)
+        warm = tile("warm", 8, F32)
+        nc.vector.memset(warm[:], 0.0)
+        for q in range(4):
+            nc.scalar.dma_start(
+                out=x_plane[32 * q : 32 * q + 4 * PASSES, :].bitcast(I32),
+                in_=x_scales[:, 4 * q : 4 * q + 4, :].bitcast(I32),
+            )
+        nc.scalar.activation(warm[:], warm[:], SILU)
+        ident = tile("ident", P, F32)
+        make_identity(nc, ident[:])
+        for q in range(4):
+            nc.gpsimd.dma_start(
+                out=w2_plane[32 * q : 32 * q + 4, :].bitcast(I32),
+                in_=w2_scales[0, 4 * q : 4 * q + 4, :].bitcast(I32),
+            )
+
+        def load_rows(name, rows):
+            raw = sb.tile([P, PACK, rows.shape[1]], F32, name=name, align_bytes=64)
+            nc.sync.dma_start(out=raw[:], in_=rows.rearrange("(p j) c -> p j c", j=PACK))
+            return raw
+
+        w1_raw, w3_raw, a_raw = {}, {}, {}
+
+        def load_weights(t):
+            cols = slice(P * t, P * (t + 1))
+            for z in range(PASSES):
+                w1_raw[t, z] = load_rows("w1_raw%d_%d" % (t, z), w1[K_PASS * z : K_PASS * (z + 1), cols])
+            w3_raw[t] = load_rows("w3_raw%d" % t, w3[:, cols])
+
+        def load_angles(c):
+            for d in range(D):
+                a_raw[c, d] = load_rows("a_raw%d_%d" % (c, d), aT[:, T * d + STARTS[c] : T * d + STARTS[c] + WIDTHS[c]])
+
+        x_flat = x_words.rearrange("z p n r -> p z (n r)")
+        x_codes = {}
+        lists = []
+        w2_codes = tile("w2_codes", N, U32)
+
+        def load_edges():
+            for half in range(HALVES):
+                for z in range(PASSES):
+                    x_codes[half, z] = tile("x_codes%d_%d" % (half, z), BANK, U32)
+                    nc.sync.dma_start(
+                        out=x_codes[half, z][:].bitcast(I32),
+                        in_=x_flat[:, z, PACK * BANK * half : PACK * BANK * (half + 1)].bitcast(I32),
+                    )
+
+        def load_lists():
+            for d, pos in enumerate((pos1, pos2)):
+                offsets = sb.tile([P, T // LIST_ROWS], U16, name="offsets%d" % d)
+                nc.sync.dma_start(offsets[:], pos)
+                lists.append(offsets)
+
+        load_weights(0)
+        load_angles(0)
+        load_edges()
+        load_lists()
+        load_weights(1)
+        load_weights(2)
+        load_weights(3)
+        load_angles(1)
+        nc.sync.dma_start(out=w2_codes[:].bitcast(I32), in_=w2_words[0].rearrange("p n r -> p (n r)").bitcast(I32))
+        load_angles(2)
+        load_angles(3)
+        load_angles(4)
+
+        def interleave(copy, grouped, raw):
+            copy(
+                out=grouped.rearrange("p (c i j) -> p c j i", i=4, j=PACK),
+                in_=raw.rearrange("p j (c i) -> p c j i", i=4),
+            )
+
+        def quantize(name, grouped):
+            width = grouped.shape[1] // PACK
+            codes = tile(name + "_codes", width, U32)
+            plane = tile(name + "_plane", width, U8)
+            nc.vector.quantize_mx(out=codes[:].bitcast(FP8X4), scales=plane[:], in_=grouped[:])
+            return codes, plane
+
+        w1_bf, w3_bf, a_bf, w1_q, w3_q, a_q = {}, {}, {}, {}, {}, {}
+        h, f, g, z_rows, z_bf, z_q = {}, {}, {}, {}, {}, {}
+
+        def cast_weights(t):
+            w1_bf[t] = tile("w1_bf%d" % t, PASSES * K_PASS, BF16)
+            for z in range(PASSES):
+                interleave(nc.vector.tensor_copy, w1_bf[t][:, K_PASS * z : K_PASS * (z + 1)], w1_raw[t, z][:])
+            w3_bf[t] = tile("w3_bf%d" % t, K_PASS, BF16)
+            interleave(nc.vector.tensor_copy if t in W3_ON_VECTOR else nc.scalar.copy, w3_bf[t][:], w3_raw[t][:])
+
+        def quantize_weights(t):
+            w3_q[t] = quantize("w3_%d" % t, w3_bf[t])
+            w1_q[t] = quantize("w1_%d" % t, w1_bf[t])
+
+        def cast_angles(c):
+            width = WIDTHS[c]
+            a_bf[c] = tile("a_bf%d" % c, D * width * PACK, BF16)
+            for d in range(D):
+                grouped = a_bf[c][:, width * PACK * d : width * PACK * (d + 1)]
+                split = min(max(ON_VECTOR[c] - width * d, 0), width)
+                if split > 0:
+                    interleave(nc.vector.tensor_copy, grouped[:, : PACK * split], a_raw[c, d][:, :, :split])
+                if split < width:
+                    interleave(nc.scalar.copy, grouped[:, PACK * split :], a_raw[c, d][:, :, split:])
+
+        def quantize_angles(c):
+            a_q[c] = quantize("a_%d" % c, a_bf[c])
+
+        def make_h(t):
+            h[t] = tile("h%d" % t, T, F32)
+            codes, plane = w1_q[t]
+            for half in range(HALVES):
+                bank = banks[2 * (t % 2) + half]
+                cols = slice(BANK * half, BANK * (half + 1))
+                for z in range(PASSES):
+                    nc.tensor.matmul_mx(
+                        out=bank[:],
+                        lhsT=codes[:, P * z : P * (z + 1)].bitcast(FP8X4),
+                        lhsT_scale=plane[:, P * z : P * (z + 1)],
+                        rhs=x_codes[half, z][:].bitcast(FP8X4),
+                        rhs_scale=x_plane[4 * z :, cols],
+                        start=(z == 0),
+                        stop=(z == PASSES - 1),
+                    )
+                nc.scalar.activation(h[t][:, cols], bank[:], SILU)
+
+        def make_f(c, t):
+            width = D * WIDTHS[c]
+            bank = banks[4 + t % 2] if c == 0 else banks[t]
+            nc.tensor.matmul_mx(
+                out=bank[:, :width],
+                lhsT=w3_q[t][0][:].bitcast(FP8X4),
+                lhsT_scale=w3_q[t][1][:],
+                rhs=a_q[c][0][:].bitcast(FP8X4),
+                rhs_scale=a_q[c][1][:],
+                start=True,
+                stop=True,
+            )
+            f[c, t] = tile("f%d_%d" % (c, t), width, F32)
+            nc.scalar.copy(out=f[c, t][:], in_=bank[:, :width])
+
+        def gather(c, t):
+            width = WIDTHS[c]
+            g[c, t] = tile("g%d_%d" % (c, t), D * width, F32)
+            entries = slice(STARTS[c] // LIST_ROWS, (STARTS[c] + width) // LIST_ROWS)
+            for d in range(D):
+                cols = slice(width * d, width * (d + 1))
+                nc.vector.tensor_tensor(g[c, t][:, cols], h[t][:].indirect(lists[d][:, entries]), f[c, t][:, cols], MULT)
+
+        def sum_z(c, b, tiles, bank):
+            width = WIDTHS[c]
+            for t in tiles:
+                for d in range(D):
+                    nc.tensor.matmul(
+                        bank[:, P * t : P * (t + 1)],
+                        g[c, t][:, width * d + P * b : width * d + P * (b + 1)],
+                        ident[:],
+                        start=(d == 0),
+                        stop=(d == D - 1),
+                        is_transpose=True,
+                    )
+            if (c, b) not in z_rows:
+                z_rows[c, b] = tile("z_rows%d_%d" % (c, b), H, BF16)
+            rows = slice(P // PACK * tiles[0], P // PACK * (tiles[-1] + 1))
+            nc.scalar.copy(
+                out=z_rows[c, b][:].rearrange("v (u p e) -> v u p e", u=2, e=2)[:, :, rows, :],
+                in_=bank[:].rearrange("v (p u e) -> v u p e", u=2, e=2)[:, :, rows, :],
+            )
+
+        def turn_z(c):
+            bank = banks[6]
+            blocks = WIDTHS[c] // P
+            for b in range(blocks):
+                words = z_rows[c, b][:].bitcast(F32)
+                for u in range(2):
+                    nc.tensor.transpose(bank[:, P * (2 * b + u) : P * (2 * b + u + 1)], words[:, P * u : P * (u + 1)], ident[:])
+            z_bf[c] = tile("z_bf%d" % c, WIDTHS[c] * PACK, BF16)
+            nc.scalar.copy(
+                out=z_bf[c][:].bitcast(F32).rearrange("p (b v u) -> p b v u", b=blocks, u=2),
+                in_=bank[:, : 2 * WIDTHS[c]].rearrange("p (b u v) -> p b v u", b=blocks, u=2),
+            )
+
+        def project(c):
+            codes, plane = quantize("z_%d" % c, z_bf[c])
+            bank = banks[7]
+            width = WIDTHS[c]
+            nc.tensor.matmul_mx(
+                out=bank[:, :width],
+                lhsT=w2_codes[:].bitcast(FP8X4),
+                lhsT_scale=w2_plane[:],
+                rhs=codes[:].bitcast(FP8X4),
+                rhs_scale=plane[:],
+                start=True,
+                stop=True,
+            )
+            result = tile("result%d" % c, width, F32)
+            nc.scalar.activation(result[:], bank[:, :width], SILU)
+            nc.sync.dma_start(out=out[:, STARTS[c] : STARTS[c] + width], in_=result[:])
+
+        cast_weights(0)
+        cast_angles(0)
+        quantize_weights(0)
+        quantize_angles(0)
+        make_f(0, 0)
+        make_h(0)
+        for t in range(TILES):
+            if t + 1 < TILES:
+                cast_weights(t + 1)
+                gather(0, t)
+                quantize_weights(t + 1)
+                make_h(t + 1)
+                make_f(0, t + 1)
+            else:
+                cast_angles(1)
+                quantize_angles(1)
+                make_f(1, 0)
+                gather(0, t)
+        every = tuple(range(TILES))
+        last = CHUNKS - 1
+        for c in range(1, CHUNKS):
+            for t in range(TILES):
+                if t + 1 < TILES:
+                    make_f(c, t + 1)
+                elif c < last:
+                    make_f(c + 1, 0)
+                if t == 0 and c < last:
+                    cast_angles(c + 1)
+                    quantize_angles(c + 1)
+                if t == 0 and c > 1:
+                    project(c - 2)
+                if 1 <= t <= WIDTHS[c - 1] // P:
+                    sum_z(c - 1, t - 1, every, banks[3 + t])
+                if t == TILES - 1:
+                    turn_z(c - 1)
+                gather(c, t)
+        project(last - 1)
+        for b in range(WIDTHS[last] // P):
+            sum_z(last, b, every[:-1], banks[b])
+            sum_z(last, b, every[-1:], banks[4 + b])
+        turn_z(last)
+        project(last)

@@ -16,6 +16,7 @@ U8 = mybir.dt.uint8
 FP8X4 = mybir.dt.float8_e4m3fn_x4
 SILU = mybir.ActivationFunctionType.Silu
 MULT = mybir.AluOpType.mult
+ADD = mybir.AluOpType.add
 
 P = 128
 PACK = 4
@@ -23,11 +24,13 @@ K_PASS = P * PACK
 BANK = 512
 PASSES = K // K_PASS
 TILES = H // P
-WIDTHS = (256,256,256,128,128)
+WIDTHS = (256,256,256,128,128,)
 STARTS = tuple(sum(WIDTHS[:c]) for c in range(len(WIDTHS)))
 CHUNKS = len(WIDTHS)
-ON_VECTOR = (256,512,0,0,0)
-W3_ON_VECTOR = ()
+ON_VECTOR = ((256,256,),(0,0,),(0,0,),(0,0,),(0,0,),)
+W_ON_VECTOR = (88,88,88,)
+ADDED = (4,)
+BY_LIST = (0,)
 HALVES = T // BANK
 LIST_ROWS = 16
 
@@ -47,14 +50,11 @@ def tile_picked_wdime_silu_l_kernel(tc, x_words, x_scales, aT, w1, w3, w2_words,
         w2_plane = tile("w2_plane", N, U8)
         nc.gpsimd.memset(x_plane[:].bitcast(U32), 0)
         nc.gpsimd.memset(w2_plane[:].bitcast(U32), 0)
-        warm = tile("warm", 8, F32)
-        nc.vector.memset(warm[:], 0.0)
         for q in range(4):
-            nc.scalar.dma_start(
+            nc.sync.dma_start(
                 out=x_plane[32 * q : 32 * q + 4 * PASSES, :].bitcast(I32),
                 in_=x_scales[:, 4 * q : 4 * q + 4, :].bitcast(I32),
             )
-        nc.scalar.activation(warm[:], warm[:], SILU)
         ident = tile("ident", P, F32)
         make_identity(nc, ident[:])
         for q in range(4):
@@ -68,50 +68,61 @@ def tile_picked_wdime_silu_l_kernel(tc, x_words, x_scales, aT, w1, w3, w2_words,
             nc.sync.dma_start(out=raw[:], in_=rows.rearrange("(p j) c -> p j c", j=PACK))
             return raw
 
-        w1_raw, w3_raw, a_raw = {}, {}, {}
-
-        def load_weights(t):
-            cols = slice(P * t, P * (t + 1))
-            for z in range(PASSES):
-                w1_raw[t, z] = load_rows("w1_raw%d_%d" % (t, z), w1[K_PASS * z : K_PASS * (z + 1), cols])
-            w3_raw[t] = load_rows("w3_raw%d" % t, w3[:, cols])
-
-        def load_angles(c):
-            for d in range(D):
-                a_raw[c, d] = load_rows("a_raw%d_%d" % (c, d), aT[:, T * d + STARTS[c] : T * d + STARTS[c] + WIDTHS[c]])
-
+        w_raw, a_raw, x_codes, lists = {}, {}, {}, []
         x_flat = x_words.rearrange("z p n r -> p z (n r)")
-        x_codes = {}
-        lists = []
         w2_codes = tile("w2_codes", N, U32)
 
-        def load_edges():
-            for half in range(HALVES):
-                for z in range(PASSES):
-                    x_codes[half, z] = tile("x_codes%d_%d" % (half, z), BANK, U32)
-                    nc.sync.dma_start(
-                        out=x_codes[half, z][:].bitcast(I32),
-                        in_=x_flat[:, z, PACK * BANK * half : PACK * BANK * (half + 1)].bitcast(I32),
-                    )
+        def load_angles(c, d):
+            a_raw[c, d] = load_rows("a_raw%d_%d" % (c, d), aT[:, T * d + STARTS[c] : T * d + STARTS[c] + WIDTHS[c]])
 
-        def load_lists():
-            for d, pos in enumerate((pos1, pos2)):
-                offsets = sb.tile([P, T // LIST_ROWS], U16, name="offsets%d" % d)
-                nc.sync.dma_start(offsets[:], pos)
-                lists.append(offsets)
+        def load_edges(half, z):
+            codes = tile("x_codes%d" % z, T, U32)
+            nc.sync.dma_start(out=codes[:].bitcast(I32), in_=x_flat[:, z, :].bitcast(I32))
+            for n in range(HALVES):
+                x_codes[n, z] = codes[:, BANK * n : BANK * (n + 1)]
 
-        load_weights(0)
-        load_angles(0)
-        load_edges()
-        load_lists()
-        load_weights(1)
-        load_weights(2)
-        load_weights(3)
-        load_angles(1)
+        def load_list(d, pos):
+            offsets = sb.tile([P, T // LIST_ROWS], U16, name="offsets%d" % d)
+            nc.sync.dma_start(offsets[:], pos)
+            lists.append(offsets)
+
+        w_raw[0] = load_rows("w1_raw0", w1[K_PASS * 0 : K_PASS * (0 + 1), :])
+        load_edges(0, 0)
+        w_raw[1] = load_rows("w1_raw1", w1[K_PASS * 1 : K_PASS * (1 + 1), :])
+        load_edges(0, 1)
+        load_list(0, pos1)
+        load_angles(0, 0)
+        w_raw[2] = load_rows("w3_raw", w3)
+        load_list(1, pos2)
+        load_angles(0, 1)
+        load_angles(1, 0)
+        load_angles(1, 1)
         nc.sync.dma_start(out=w2_codes[:].bitcast(I32), in_=w2_words[0].rearrange("p n r -> p (n r)").bitcast(I32))
-        load_angles(2)
-        load_angles(3)
-        load_angles(4)
+        load_angles(2, 0)
+        load_angles(2, 1)
+        load_angles(3, 0)
+        load_angles(3, 1)
+        load_angles(4, 0)
+        load_angles(4, 1)
+
+        def quantize(name, grouped):
+            width = grouped.shape[1] // PACK
+            codes = tile(name + "_codes", width, U32)
+            plane = tile(name + "_plane", width, U8)
+            nc.vector.quantize_mx(out=codes[:].bitcast(FP8X4), scales=plane[:], in_=grouped)
+            return codes, plane
+
+        w_q, a_bf, a_q = {}, {}, {}
+        h, f, g, z_rows, z_bf = {}, {}, {}, {}, {}
+
+        def prepare_weights(n, pieces):
+            source = w_raw[n][:].rearrange("p j (m t) -> p m j t", t=TILES)
+            for first, count, copy in pieces:
+                grouped = tile("w_bf%d_%d" % (n, first), count * P * PACK, BF16)
+                copy(out=grouped[:].rearrange("p (t m j) -> p m j t", t=count, j=PACK), in_=source[:, :, :, first : first + count])
+                codes, plane = quantize("w_%d_%d" % (n, first), grouped[:])
+                for t in range(count):
+                    w_q[n, first + t] = (codes[:, P * t : P * (t + 1)], plane[:, P * t : P * (t + 1)])
 
         def interleave(copy, grouped, raw):
             copy(
@@ -119,119 +130,107 @@ def tile_picked_wdime_silu_l_kernel(tc, x_words, x_scales, aT, w1, w3, w2_words,
                 in_=raw.rearrange("p j (c i) -> p c j i", i=4),
             )
 
-        def quantize(name, grouped):
-            width = grouped.shape[1] // PACK
-            codes = tile(name + "_codes", width, U32)
-            plane = tile(name + "_plane", width, U8)
-            nc.vector.quantize_mx(out=codes[:].bitcast(FP8X4), scales=plane[:], in_=grouped[:])
-            return codes, plane
+        def parts(c):
+            return [(d,) for d in range(D)] if c in BY_LIST else [tuple(range(D))]
 
-        w1_bf, w3_bf, a_bf, w1_q, w3_q, a_q = {}, {}, {}, {}, {}, {}
-        h, f, g, z_rows, z_bf, z_q = {}, {}, {}, {}, {}, {}
-
-        def cast_weights(t):
-            w1_bf[t] = tile("w1_bf%d" % t, PASSES * K_PASS, BF16)
-            for z in range(PASSES):
-                interleave(nc.vector.tensor_copy, w1_bf[t][:, K_PASS * z : K_PASS * (z + 1)], w1_raw[t, z][:])
-            w3_bf[t] = tile("w3_bf%d" % t, K_PASS, BF16)
-            interleave(nc.vector.tensor_copy if t in W3_ON_VECTOR else nc.scalar.copy, w3_bf[t][:], w3_raw[t][:])
-
-        def quantize_weights(t):
-            w3_q[t] = quantize("w3_%d" % t, w3_bf[t])
-            w1_q[t] = quantize("w1_%d" % t, w1_bf[t])
-
-        def cast_angles(c):
+        def prepare_angles(c, part):
             width = WIDTHS[c]
-            a_bf[c] = tile("a_bf%d" % c, D * width * PACK, BF16)
-            for d in range(D):
-                grouped = a_bf[c][:, width * PACK * d : width * PACK * (d + 1)]
-                split = min(max(ON_VECTOR[c] - width * d, 0), width)
+            grouped = tile("a_bf%d_%d" % (c, part[0]), len(part) * width * PACK, BF16)
+            for n, d in enumerate(part):
+                piece = grouped[:, width * PACK * n : width * PACK * (n + 1)]
+                split = ON_VECTOR[c][d]
                 if split > 0:
-                    interleave(nc.vector.tensor_copy, grouped[:, : PACK * split], a_raw[c, d][:, :, :split])
+                    interleave(nc.vector.tensor_copy, piece[:, : PACK * split], a_raw[c, d][:, :, :split])
                 if split < width:
-                    interleave(nc.scalar.copy, grouped[:, PACK * split :], a_raw[c, d][:, :, split:])
+                    interleave(nc.scalar.copy, piece[:, PACK * split :], a_raw[c, d][:, :, split:])
+            a_q[c, part] = quantize("a_%d_%d" % (c, part[0]), grouped[:])
 
-        def quantize_angles(c):
-            a_q[c] = quantize("a_%d" % c, a_bf[c])
+        def make_h(t, half):
+            bank = banks[(2 * t + half) % 6]
+            cols = slice(BANK * half, BANK * (half + 1))
+            if half == 0:
+                h[t] = tile("h%d" % t, T, F32)
+            for z in range(PASSES):
+                nc.tensor.matmul_mx(
+                    out=bank[:],
+                    lhsT=w_q[z, t][0].bitcast(FP8X4),
+                    lhsT_scale=w_q[z, t][1],
+                    rhs=x_codes[half, z].bitcast(FP8X4),
+                    rhs_scale=x_plane[4 * z :, cols],
+                    start=(z == 0),
+                    stop=(z == PASSES - 1),
+                )
+            nc.scalar.activation(h[t][:, cols], bank[:], SILU)
 
-        def make_h(t):
-            h[t] = tile("h%d" % t, T, F32)
-            codes, plane = w1_q[t]
-            for half in range(HALVES):
-                bank = banks[2 * (t % 2) + half]
-                cols = slice(BANK * half, BANK * (half + 1))
-                for z in range(PASSES):
-                    nc.tensor.matmul_mx(
-                        out=bank[:],
-                        lhsT=codes[:, P * z : P * (z + 1)].bitcast(FP8X4),
-                        lhsT_scale=plane[:, P * z : P * (z + 1)],
-                        rhs=x_codes[half, z][:].bitcast(FP8X4),
-                        rhs_scale=x_plane[4 * z :, cols],
-                        start=(z == 0),
-                        stop=(z == PASSES - 1),
-                    )
-                nc.scalar.activation(h[t][:, cols], bank[:], SILU)
+        def make_f(c, part, tiles, bank, copy=nc.scalar.copy):
+            width = len(part) * WIDTHS[c]
+            codes, plane = a_q[c, part]
+            for n, t in enumerate(tiles):
+                nc.tensor.matmul_mx(
+                    out=bank[:, width * n : width * (n + 1)],
+                    lhsT=w_q[2, t][0].bitcast(FP8X4),
+                    lhsT_scale=w_q[2, t][1],
+                    rhs=codes[:].bitcast(FP8X4),
+                    rhs_scale=plane[:],
+                    start=True,
+                    stop=True,
+                )
+            filters = tile("f%d_%d_%d" % (c, part[0], tiles[0]), width * len(tiles), F32)
+            copy(out=filters[:], in_=bank[:, : width * len(tiles)])
+            for n, t in enumerate(tiles):
+                for i, d in enumerate(part):
+                    f[c, t, d] = filters[:, width * n + WIDTHS[c] * i : width * n + WIDTHS[c] * (i + 1)]
 
-        def make_f(c, t):
-            width = D * WIDTHS[c]
-            bank = banks[4 + t % 2] if c == 0 else banks[t]
-            nc.tensor.matmul_mx(
-                out=bank[:, :width],
-                lhsT=w3_q[t][0][:].bitcast(FP8X4),
-                lhsT_scale=w3_q[t][1][:],
-                rhs=a_q[c][0][:].bitcast(FP8X4),
-                rhs_scale=a_q[c][1][:],
-                start=True,
-                stop=True,
-            )
-            f[c, t] = tile("f%d_%d" % (c, t), width, F32)
-            nc.scalar.copy(out=f[c, t][:], in_=bank[:, :width])
-
-        def gather(c, t):
+        def gather(c, t, d):
             width = WIDTHS[c]
-            g[c, t] = tile("g%d_%d" % (c, t), D * width, F32)
+            if (c, d) not in g:
+                g[c, d] = sb.tile([P, TILES, width], F32, name="g%d_%d" % (c, d), align_bytes=64)
             entries = slice(STARTS[c] // LIST_ROWS, (STARTS[c] + width) // LIST_ROWS)
-            for d in range(D):
-                cols = slice(width * d, width * (d + 1))
-                nc.vector.tensor_tensor(g[c, t][:, cols], h[t][:].indirect(lists[d][:, entries]), f[c, t][:, cols], MULT)
+            nc.vector.tensor_tensor(g[c, d][:, t, :], h[t][:].indirect(lists[d][:, entries]), f[c, t, d], MULT)
 
-        def sum_z(c, b, tiles, bank):
-            width = WIDTHS[c]
-            for t in tiles:
+        def sum_z(c, b):
+            bank = banks[4 + b % 2]
+            for t in range(TILES):
                 for d in range(D):
                     nc.tensor.matmul(
                         bank[:, P * t : P * (t + 1)],
-                        g[c, t][:, width * d + P * b : width * d + P * (b + 1)],
+                        g[c, d][:, t, P * b : P * (b + 1)],
                         ident[:],
                         start=(d == 0),
                         stop=(d == D - 1),
                         is_transpose=True,
                     )
-            if (c, b) not in z_rows:
-                z_rows[c, b] = tile("z_rows%d_%d" % (c, b), H, BF16)
-            rows = slice(P // PACK * tiles[0], P // PACK * (tiles[-1] + 1))
+            z_rows[c, b] = tile("z_rows%d_%d" % (c, b), H, BF16)
             nc.scalar.copy(
-                out=z_rows[c, b][:].rearrange("v (u p e) -> v u p e", u=2, e=2)[:, :, rows, :],
-                in_=bank[:].rearrange("v (p u e) -> v u p e", u=2, e=2)[:, :, rows, :],
+                out=z_rows[c, b][:].rearrange("v (u p e) -> v u p e", u=2, e=2),
+                in_=bank[:].rearrange("v (u e p) -> v u p e", u=2, e=2),
             )
 
-        def turn_z(c):
+        def turn_z(c, blocks):
             bank = banks[6]
-            blocks = WIDTHS[c] // P
-            for b in range(blocks):
+            for n, b in enumerate(blocks):
                 words = z_rows[c, b][:].bitcast(F32)
                 for u in range(2):
-                    nc.tensor.transpose(bank[:, P * (2 * b + u) : P * (2 * b + u + 1)], words[:, P * u : P * (u + 1)], ident[:])
-            z_bf[c] = tile("z_bf%d" % c, WIDTHS[c] * PACK, BF16)
+                    nc.tensor.transpose(bank[:, P * (2 * n + u) : P * (2 * n + u + 1)], words[:, P * u : P * (u + 1)], ident[:])
+            z_bf[c, blocks[0]] = tile("z_bf%d_%d" % (c, blocks[0]), len(blocks) * P * PACK, BF16)
             nc.scalar.copy(
-                out=z_bf[c][:].bitcast(F32).rearrange("p (b v u) -> p b v u", b=blocks, u=2),
-                in_=bank[:, : 2 * WIDTHS[c]].rearrange("p (b u v) -> p b v u", b=blocks, u=2),
+                out=z_bf[c, blocks[0]][:].bitcast(F32).rearrange("p (b v u) -> p b v u", b=len(blocks), u=2),
+                in_=bank[:, : 2 * P * len(blocks)].rearrange("p (b u v) -> p b v u", b=len(blocks), u=2),
             )
 
-        def project(c):
-            codes, plane = quantize("z_%d" % c, z_bf[c])
-            bank = banks[7]
-            width = WIDTHS[c]
+        def add_z(c):
+            z_bf[c, 0] = tile("z_bf%d_0" % c, WIDTHS[c] * PACK, BF16)
+            nc.vector.tensor_tensor(
+                z_bf[c, 0][:].rearrange("p (c i t) -> p c t i", i=4, t=TILES),
+                g[c, 0][:].rearrange("p t (c i) -> p c t i", i=4),
+                g[c, 1][:].rearrange("p t (c i) -> p c t i", i=4),
+                ADD,
+            )
+
+        def project(c, b):
+            codes, plane = quantize("z_%d_%d" % (c, b), z_bf[c, b][:])
+            bank = banks[4 + c % 2] if c in ADDED else banks[7]
+            width = codes.shape[1]
             nc.tensor.matmul_mx(
                 out=bank[:, :width],
                 lhsT=w2_codes[:].bitcast(FP8X4),
@@ -241,49 +240,52 @@ def tile_picked_wdime_silu_l_kernel(tc, x_words, x_scales, aT, w1, w3, w2_words,
                 start=True,
                 stop=True,
             )
-            result = tile("result%d" % c, width, F32)
+            result = tile("result%d_%d" % (c, b), width, F32)
             nc.scalar.activation(result[:], bank[:, :width], SILU)
-            nc.sync.dma_start(out=out[:, STARTS[c] : STARTS[c] + width], in_=result[:])
+            nc.sync.dma_start(out=out[:, STARTS[c] + P * b : STARTS[c] + P * b + width], in_=result[:])
 
-        cast_weights(0)
-        cast_angles(0)
-        quantize_weights(0)
-        quantize_angles(0)
-        make_f(0, 0)
-        make_h(0)
-        for t in range(TILES):
-            if t + 1 < TILES:
-                cast_weights(t + 1)
-                gather(0, t)
-                quantize_weights(t + 1)
-                make_h(t + 1)
-                make_f(0, t + 1)
-            else:
-                cast_angles(1)
-                quantize_angles(1)
-                make_f(1, 0)
-                gather(0, t)
-        every = tuple(range(TILES))
-        last = CHUNKS - 1
-        for c in range(1, CHUNKS):
+        units = [(c, part) for c in range(CHUNKS) for part in parts(c)]
+
+        def filter_steps(c, part):
+            per_bank = BANK // (len(part) * WIDTHS[c])
+            return [tuple(range(t, min(t + per_bank, TILES))) for t in range(0, TILES, per_bank)]
+
+        prepare_weights(0, [(0, 4, nc.vector.tensor_copy)])
+        prepare_weights(1, [(0, 2, nc.vector.tensor_copy), (2, 2, nc.vector.tensor_copy)])
+        prepare_angles(*units[0])
+        prepare_weights(2, [(0, 2, nc.vector.tensor_copy), (2, 2, nc.vector.tensor_copy)])
+        for n, tiles in enumerate(filter_steps(*units[0])):
+            make_f(*units[0], tiles, banks[7 - n], nc.scalar.copy)
+        ring = 0
+        projected = 0
+        for u, (c, part) in enumerate(units):
+            coming = units[u + 1] if u + 1 < len(units) else None
+            own = filter_steps(c, part)[1:] if u > 0 else []
+            before = c - 1
             for t in range(TILES):
-                if t + 1 < TILES:
-                    make_f(c, t + 1)
-                elif c < last:
-                    make_f(c + 1, 0)
-                if t == 0 and c < last:
-                    cast_angles(c + 1)
-                    quantize_angles(c + 1)
-                if t == 0 and c > 1:
-                    project(c - 2)
-                if 1 <= t <= WIDTHS[c - 1] // P:
-                    sum_z(c - 1, t - 1, every, banks[3 + t])
-                if t == TILES - 1:
-                    turn_z(c - 1)
-                gather(c, t)
-        project(last - 1)
-        for b in range(WIDTHS[last] // P):
-            sum_z(last, b, every[:-1], banks[b])
-            sum_z(last, b, every[-1:], banks[4 + b])
-        turn_z(last)
-        project(last)
+                if u == 0:
+                    for half in range(HALVES):
+                        make_h(t, half)
+                if own and own[0][0] <= t + 1:
+                    make_f(c, part, own.pop(0), banks[ring % 4])
+                    ring = ring + 1
+                if coming and t == 0:
+                    prepare_angles(*coming)
+                if coming and t == TILES - 1:
+                    make_f(*coming, filter_steps(*coming)[0], banks[ring % 4])
+                    ring = ring + 1
+                if before >= 0 and before not in ADDED:
+                    blocks = tuple(range(WIDTHS[before] // P))
+                    if t - 1 in blocks:
+                        sum_z(before, t - 1)
+                    if t == TILES - 1:
+                        turn_z(before, blocks)
+                if t == 3 and c >= 2 and u > 0:
+                    project(c - 2, 0)
+                    projected = c - 1
+                for d in part:
+                    gather(c, t, d)
+            if c in ADDED:
+                add_z(c)
+        for c in range(projected, CHUNKS):
+            project(c, 0)

from contextlib import ExitStack

import concourse.mybir as mybir
from concourse.masks import make_identity

K, T, H, N, J = 1024, 1024, 512, 128, 512
D = 2
FLOPS = 2 * (K * H * T + J * H * D * T + H * N * T)

F32 = mybir.dt.float32
BF16 = mybir.dt.bfloat16
I32 = mybir.dt.int32
U32 = mybir.dt.uint32
U16 = mybir.dt.uint16
U8 = mybir.dt.uint8
FP8X4 = mybir.dt.float8_e4m3fn_x4
SILU = mybir.ActivationFunctionType.Silu
MULT = mybir.AluOpType.mult
ADD = mybir.AluOpType.add

P = 128
PACK = 4
K_PASS = P * PACK
BANK = 512
PASSES = K // K_PASS
TILES = H // P
WIDTHS = (256,256,256,128,128,)
STARTS = tuple(sum(WIDTHS[:c]) for c in range(len(WIDTHS)))
CHUNKS = len(WIDTHS)
ON_VECTOR = ((256,256,),(0,0,),(0,0,),(0,0,),(0,0,),)
W_ON_VECTOR = (88,88,88,)
ADDED = (4,)
BY_LIST = (0,)
HALVES = T // BANK
LIST_ROWS = 16


def tile_picked_wdime_silu_l_kernel(tc, x_words, x_scales, aT, w1, w3, w2_words, w2_scales, pos1, pos2, out):
    nc = tc.nc
    with ExitStack() as ctx:
        sb = ctx.enter_context(tc.tile_pool(name="sb", bufs=1))
        ps = ctx.enter_context(tc.psum_pool(name="ps", bufs=1))

        def tile(name, width, dtype):
            return sb.tile([P, width], dtype, name=name, align_bytes=64)

        banks = [ps.tile([P, BANK], F32, name="bank%d" % b) for b in range(8)]

        x_plane = tile("x_plane", T, U8)
        w2_plane = tile("w2_plane", N, U8)
        nc.gpsimd.memset(x_plane[:].bitcast(U32), 0)
        nc.gpsimd.memset(w2_plane[:].bitcast(U32), 0)
        for q in range(4):
            nc.sync.dma_start(
                out=x_plane[32 * q : 32 * q + 4 * PASSES, :].bitcast(I32),
                in_=x_scales[:, 4 * q : 4 * q + 4, :].bitcast(I32),
            )
        ident = tile("ident", P, F32)
        make_identity(nc, ident[:])
        for q in range(4):
            nc.gpsimd.dma_start(
                out=w2_plane[32 * q : 32 * q + 4, :].bitcast(I32),
                in_=w2_scales[0, 4 * q : 4 * q + 4, :].bitcast(I32),
            )

        def load_rows(name, rows):
            raw = sb.tile([P, PACK, rows.shape[1]], F32, name=name, align_bytes=64)
            nc.sync.dma_start(out=raw[:], in_=rows.rearrange("(p j) c -> p j c", j=PACK))
            return raw

        w_raw, a_raw, x_codes, lists = {}, {}, {}, []
        x_flat = x_words.rearrange("z p n r -> p z (n r)")
        w2_codes = tile("w2_codes", N, U32)

        def load_angles(c, d):
            a_raw[c, d] = load_rows("a_raw%d_%d" % (c, d), aT[:, T * d + STARTS[c] : T * d + STARTS[c] + WIDTHS[c]])

        def load_edges(half, z):
            codes = tile("x_codes%d" % z, T, U32)
            nc.sync.dma_start(out=codes[:].bitcast(I32), in_=x_flat[:, z, :].bitcast(I32))
            for n in range(HALVES):
                x_codes[n, z] = codes[:, BANK * n : BANK * (n + 1)]

        def load_list(d, pos):
            offsets = sb.tile([P, T // LIST_ROWS], U16, name="offsets%d" % d)
            nc.sync.dma_start(offsets[:], pos)
            lists.append(offsets)

        w_raw[0] = load_rows("w1_raw0", w1[K_PASS * 0 : K_PASS * (0 + 1), :])
        load_edges(0, 0)
        w_raw[1] = load_rows("w1_raw1", w1[K_PASS * 1 : K_PASS * (1 + 1), :])
        load_edges(0, 1)
        load_list(0, pos1)
        load_angles(0, 0)
        w_raw[2] = load_rows("w3_raw", w3)
        load_list(1, pos2)
        load_angles(0, 1)
        load_angles(1, 0)
        load_angles(1, 1)
        nc.sync.dma_start(out=w2_codes[:].bitcast(I32), in_=w2_words[0].rearrange("p n r -> p (n r)").bitcast(I32))
        load_angles(2, 0)
        load_angles(2, 1)
        load_angles(3, 0)
        load_angles(3, 1)
        load_angles(4, 0)
        load_angles(4, 1)

        def quantize(name, grouped):
            width = grouped.shape[1] // PACK
            codes = tile(name + "_codes", width, U32)
            plane = tile(name + "_plane", width, U8)
            nc.vector.quantize_mx(out=codes[:].bitcast(FP8X4), scales=plane[:], in_=grouped)
            return codes, plane

        w_q, a_bf, a_q = {}, {}, {}
        h, f, g, z_rows, z_bf = {}, {}, {}, {}, {}

        def prepare_weights(n, pieces):
            source = w_raw[n][:].rearrange("p j (m t) -> p m j t", t=TILES)
            for first, count, copy in pieces:
                grouped = tile("w_bf%d_%d" % (n, first), count * P * PACK, BF16)
                copy(out=grouped[:].rearrange("p (t m j) -> p m j t", t=count, j=PACK), in_=source[:, :, :, first : first + count])
                codes, plane = quantize("w_%d_%d" % (n, first), grouped[:])
                for t in range(count):
                    w_q[n, first + t] = (codes[:, P * t : P * (t + 1)], plane[:, P * t : P * (t + 1)])

        def interleave(copy, grouped, raw):
            copy(
                out=grouped.rearrange("p (c i j) -> p c j i", i=4, j=PACK),
                in_=raw.rearrange("p j (c i) -> p c j i", i=4),
            )

        def parts(c):
            return [(d,) for d in range(D)] if c in BY_LIST else [tuple(range(D))]

        def prepare_angles(c, part):
            width = WIDTHS[c]
            grouped = tile("a_bf%d_%d" % (c, part[0]), len(part) * width * PACK, BF16)
            for n, d in enumerate(part):
                piece = grouped[:, width * PACK * n : width * PACK * (n + 1)]
                split = ON_VECTOR[c][d]
                if split > 0:
                    interleave(nc.vector.tensor_copy, piece[:, : PACK * split], a_raw[c, d][:, :, :split])
                if split < width:
                    interleave(nc.scalar.copy, piece[:, PACK * split :], a_raw[c, d][:, :, split:])
            a_q[c, part] = quantize("a_%d_%d" % (c, part[0]), grouped[:])

        def make_h(t, half):
            bank = banks[(2 * t + half) % 6]
            cols = slice(BANK * half, BANK * (half + 1))
            if half == 0:
                h[t] = tile("h%d" % t, T, F32)
            for z in range(PASSES):
                nc.tensor.matmul_mx(
                    out=bank[:],
                    lhsT=w_q[z, t][0].bitcast(FP8X4),
                    lhsT_scale=w_q[z, t][1],
                    rhs=x_codes[half, z].bitcast(FP8X4),
                    rhs_scale=x_plane[4 * z :, cols],
                    start=(z == 0),
                    stop=(z == PASSES - 1),
                )
            nc.scalar.activation(h[t][:, cols], bank[:], SILU)

        def make_f(c, part, tiles, bank, copy=nc.scalar.copy):
            width = len(part) * WIDTHS[c]
            codes, plane = a_q[c, part]
            for n, t in enumerate(tiles):
                nc.tensor.matmul_mx(
                    out=bank[:, width * n : width * (n + 1)],
                    lhsT=w_q[2, t][0].bitcast(FP8X4),
                    lhsT_scale=w_q[2, t][1],
                    rhs=codes[:].bitcast(FP8X4),
                    rhs_scale=plane[:],
                    start=True,
                    stop=True,
                )
            filters = tile("f%d_%d_%d" % (c, part[0], tiles[0]), width * len(tiles), F32)
            copy(out=filters[:], in_=bank[:, : width * len(tiles)])
            for n, t in enumerate(tiles):
                for i, d in enumerate(part):
                    f[c, t, d] = filters[:, width * n + WIDTHS[c] * i : width * n + WIDTHS[c] * (i + 1)]

        def gather(c, t, d):
            width = WIDTHS[c]
            if (c, d) not in g:
                g[c, d] = sb.tile([P, TILES, width], F32, name="g%d_%d" % (c, d), align_bytes=64)
            entries = slice(STARTS[c] // LIST_ROWS, (STARTS[c] + width) // LIST_ROWS)
            nc.vector.tensor_tensor(g[c, d][:, t, :], h[t][:].indirect(lists[d][:, entries]), f[c, t, d], MULT)

        def sum_z(c, b):
            bank = banks[4 + b % 2]
            for t in range(TILES):
                for d in range(D):
                    nc.tensor.matmul(
                        bank[:, P * t : P * (t + 1)],
                        g[c, d][:, t, P * b : P * (b + 1)],
                        ident[:],
                        start=(d == 0),
                        stop=(d == D - 1),
                        is_transpose=True,
                    )
            z_rows[c, b] = tile("z_rows%d_%d" % (c, b), H, BF16)
            nc.scalar.copy(
                out=z_rows[c, b][:].rearrange("v (u p e) -> v u p e", u=2, e=2),
                in_=bank[:].rearrange("v (u e p) -> v u p e", u=2, e=2),
            )

        def turn_z(c, blocks):
            bank = banks[6]
            for n, b in enumerate(blocks):
                words = z_rows[c, b][:].bitcast(F32)
                for u in range(2):
                    nc.tensor.transpose(bank[:, P * (2 * n + u) : P * (2 * n + u + 1)], words[:, P * u : P * (u + 1)], ident[:])
            z_bf[c, blocks[0]] = tile("z_bf%d_%d" % (c, blocks[0]), len(blocks) * P * PACK, BF16)
            nc.scalar.copy(
                out=z_bf[c, blocks[0]][:].bitcast(F32).rearrange("p (b v u) -> p b v u", b=len(blocks), u=2),
                in_=bank[:, : 2 * P * len(blocks)].rearrange("p (b u v) -> p b v u", b=len(blocks), u=2),
            )

        def add_z(c):
            z_bf[c, 0] = tile("z_bf%d_0" % c, WIDTHS[c] * PACK, BF16)
            nc.vector.tensor_tensor(
                z_bf[c, 0][:].rearrange("p (c i t) -> p c t i", i=4, t=TILES),
                g[c, 0][:].rearrange("p t (c i) -> p c t i", i=4),
                g[c, 1][:].rearrange("p t (c i) -> p c t i", i=4),
                ADD,
            )

        def project(c, b):
            codes, plane = quantize("z_%d_%d" % (c, b), z_bf[c, b][:])
            bank = banks[4 + c % 2] if c in ADDED else banks[7]
            width = codes.shape[1]
            nc.tensor.matmul_mx(
                out=bank[:, :width],
                lhsT=w2_codes[:].bitcast(FP8X4),
                lhsT_scale=w2_plane[:],
                rhs=codes[:].bitcast(FP8X4),
                rhs_scale=plane[:],
                start=True,
                stop=True,
            )
            result = tile("result%d_%d" % (c, b), width, F32)
            nc.scalar.activation(result[:], bank[:, :width], SILU)
            nc.sync.dma_start(out=out[:, STARTS[c] + P * b : STARTS[c] + P * b + width], in_=result[:])

        units = [(c, part) for c in range(CHUNKS) for part in parts(c)]

        def filter_steps(c, part):
            per_bank = BANK // (len(part) * WIDTHS[c])
            return [tuple(range(t, min(t + per_bank, TILES))) for t in range(0, TILES, per_bank)]

        prepare_weights(0, [(0, 4, nc.vector.tensor_copy)])
        prepare_weights(1, [(0, 2, nc.vector.tensor_copy), (2, 2, nc.vector.tensor_copy)])
        prepare_angles(*units[0])
        prepare_weights(2, [(0, 2, nc.vector.tensor_copy), (2, 2, nc.vector.tensor_copy)])
        for n, tiles in enumerate(filter_steps(*units[0])):
            make_f(*units[0], tiles, banks[7 - n], nc.scalar.copy)
        ring = 0
        projected = 0
        for u, (c, part) in enumerate(units):
            coming = units[u + 1] if u + 1 < len(units) else None
            own = filter_steps(c, part)[1:] if u > 0 else []
            before = c - 1
            for t in range(TILES):
                if u == 0:
                    for half in range(HALVES):
                        make_h(t, half)
                if own and own[0][0] <= t + 1:
                    make_f(c, part, own.pop(0), banks[ring % 4])
                    ring = ring + 1
                if coming and t == 0:
                    prepare_angles(*coming)
                if coming and t == TILES - 1:
                    make_f(*coming, filter_steps(*coming)[0], banks[ring % 4])
                    ring = ring + 1
                if before >= 0 and before not in ADDED:
                    blocks = tuple(range(WIDTHS[before] // P))
                    if t - 1 in blocks:
                        sum_z(before, t - 1)
                    if t == TILES - 1:
                        turn_z(before, blocks)
                if t == 3 and c >= 2 and u > 0:
                    project(c - 2, 0)
                    projected = c - 1
                for d in part:
                    gather(c, t, d)
            if c in ADDED:
                add_z(c)
        for c in range(projected, CHUNKS):
            project(c, 0)
